import numpy as np
import ml_dtypes


def mxq(x, axis, fmt="e4m3"):
    dtype, down = {"e4m3": (ml_dtypes.float8_e4m3fn, 7), "e5m2": (ml_dtypes.float8_e5m2, 14)}[fmt]
    v = np.moveaxis(np.asarray(x, np.float32).astype(ml_dtypes.bfloat16).astype(np.float64), axis, -1)
    blocks = v.reshape(v.shape[:-1] + (-1, 32))
    amax = np.abs(blocks).max(-1, keepdims=True)
    byte = np.maximum(np.where(amax > 0, np.frexp(amax)[1] - 1 + 127, 0) - down, 1)
    scale = np.exp2(byte - 127.0)
    codes = (blocks / scale).astype(np.float32).astype(dtype).astype(np.float64)
    return np.moveaxis((codes * scale).reshape(v.shape), -1, axis)


WIDE = False


def mx_kscale(k):
    if not WIDE:
        return np.ones(k)
    levels = np.array([10, -10, 5, -5, 0])
    if k % 512:
        return np.exp2(np.random.permutation(np.resize(levels, k // 32))).repeat(32)
    a = np.empty((k // 512, 16))
    for p in range(k // 512):
        a[p, :8] = np.random.permutation(np.resize(levels, 8))
        for g in range(8):
            far = levels[np.abs(levels - a[p, g]) >= 10]
            a[p, g + 8] = far[np.random.randint(len(far))]
    return np.exp2(a.ravel()).repeat(32)


def f64(x):
    return np.asarray(x).astype(np.float64)


def striped8(idx):
    return np.asarray(idx).reshape(8, -1, 16).transpose(0, 2, 1).reshape(128, -1).astype(np.uint16)


def unstriped8(offs):
    return offs.reshape(8, 16, -1).transpose(0, 2, 1).reshape(8, -1).astype(np.int64)


def pick8(x, idx, run):
    r = np.arange(len(x))
    return x[r[:, None], idx[r % (8 * run) // run]]


E2M1 = np.array([0.0, 0.5, 1.0, 1.5, 2.0, 3.0, 4.0, 6.0, -0.0, -0.5, -1.0, -1.5, -2.0, -3.0, -4.0, -6.0])


def pack_weight(w, fmt):
    k, n = w.shape
    w = f64(np.asarray(w, np.float32).astype(ml_dtypes.bfloat16)).reshape(k // 32, 32, n)
    amax = np.abs(w).max(1)
    if fmt == "e4m3":
        byte = np.frexp(amax)[1] - 1 + 127 - 7
    else:
        mant, ex = np.frexp(amax / 6.0)
        byte = np.where(mant > 0.5, ex, ex - 1) + 127
    byte = np.clip(np.where(amax > 0, byte, 1), 1, 254)
    scaled = (w * np.exp2(127.0 - byte)[:, None, :]).reshape(k, n).astype(np.float32)
    by_word = np.ascontiguousarray(scaled.reshape(k // 512, 128, 4, n).transpose(0, 1, 3, 2))
    if fmt == "e4m3":
        words = by_word.astype(ml_dtypes.float8_e4m3fn).view(np.uint8)
    else:
        c = by_word.astype(ml_dtypes.float4_e2m1fn).view(np.uint8) & 0xF
        words = (c[..., 0::2] | (c[..., 1::2] << 4)).reshape(k // 512, 128, 2 * n)
    return np.ascontiguousarray(words), np.ascontiguousarray(byte.astype(np.uint8).reshape(k // 512, 16, n))


def unpack_weight(words, scales, fmt):
    g, _, n = scales.shape
    words = np.ascontiguousarray(words).reshape(g, 128, n, -1)
    if fmt == "e4m3":
        vals = words.view(ml_dtypes.float8_e4m3fn).astype(np.float64)
    else:
        nib = np.empty((g, 128, n, 4), np.uint8)
        nib[..., 0::2] = words & 0xF
        nib[..., 1::2] = words >> 4
        vals = E2M1[nib]
    vals = vals * np.repeat(np.exp2(scales.astype(np.float64) - 127.0), 8, axis=1)[..., None]
    return vals.transpose(0, 1, 3, 2).reshape(g * 512, n)


D, T, U, X, I, Q = 512, 1024, 1024, 1024, 512, 128


def setup_inputs():
    n = np.random.standard_normal
    idx = np.stack([np.random.permutation(T)[:I] for _ in range(8)])
    idx2 = np.stack([np.random.permutation(U)[:I] for _ in range(8)])
    idx3 = np.stack([np.random.permutation(X)[:I] for _ in range(8)])
    idx4 = np.stack([np.random.permutation(X)[:I] for _ in range(8)])
    fd = mx_kscale(D)
    keysp = pack_weight(n((D, T)) / fd[:, None], "e2m1")
    notesp = pack_weight(n((D, U)) / fd[:, None], "e4m3")
    usersp = pack_weight(n((D, X)) / fd[:, None], "e2m1")
    return {
        "query": (n((D, Q)) * 1.0 / np.sqrt(D) * fd[:, None]).astype(np.float32),
        "keys_words": keysp[0],
        "keys_scales": keysp[1],
        "notes_words": notesp[0],
        "notes_scales": notesp[1],
        "users_words": usersp[0],
        "users_scales": usersp[1],
        "offs": striped8(idx),
        "offs2": striped8(idx2),
        "offs3": striped8(idx3),
        "offs4": striped8(idx4),
    }


def reference(query, keys_words, keys_scales, notes_words, notes_scales, users_words, users_scales, offs, offs2, offs3, offs4):
    idx = unstriped8(offs)
    idx2 = unstriped8(offs2)
    idx3 = unstriped8(offs3)
    idx4 = unstriped8(offs4)
    keysu = unpack_weight(keys_words, keys_scales, "e2m1")
    notesu = unpack_weight(notes_words, notes_scales, "e4m3")
    usersu = unpack_weight(users_words, users_scales, "e2m1")
    queryq = mxq(f64(query), 0, "e4m3")
    a = queryq.T @ keysu
    b = queryq.T @ notesu
    c0 = queryq.T @ usersu
    lo1 = np.minimum(pick8(a, idx, 16), pick8(b, idx2, 16))
    hi1 = np.maximum(pick8(a, idx, 16), pick8(b, idx2, 16))
    w = np.maximum(lo1, np.minimum(hi1, pick8(c0, idx3, 16)))
    f1 = np.zeros((Q, X))
    f1[np.arange(Q)[:, None], idx3[np.arange(Q) % 128 // 16]] = w
    cc = c0 - f1
    y = pick8(cc, idx4, 16) + w
    return y

@@ -1,0 +1,149 @@
+from contextlib import ExitStack
+
+import concourse.mybir as mybir
+
+D, POOL, SLOTS, Q = 512, 1024, 512, 128
+FLOPS = 3 * 2 * D * Q * POOL
+
+F32 = mybir.dt.float32
+BF16 = mybir.dt.bfloat16
+I32 = mybir.dt.int32
+U32 = mybir.dt.uint32
+U16 = mybir.dt.uint16
+U8 = mybir.dt.uint8
+FP8X4 = mybir.dt.float8_e4m3fn_x4
+FP4X4 = mybir.dt.float4_e2m1fn_x4
+COPY = mybir.ActivationFunctionType.Copy
+ALU = mybir.AluOpType
+
+P = 128
+PACK = 4
+BANK = 512
+HALF = SLOTS // 2
+LIST_COLS = HALF // 16
+
+
+def tile_attend_middleone_three_kernel(tc, query, keys_words, keys_scales, notes_words, notes_scales,
+                                        users_words, users_scales, offs, offs2, offs3, offs4, out):
+    nc = tc.nc
+    with ExitStack() as ctx:
+        sb = ctx.enter_context(tc.tile_pool(name="sb", bufs=1))
+        ps = ctx.enter_context(tc.psum_pool(name="ps", bufs=1))
+
+        lists = [sb.tile([P, SLOTS // 16], U16, name=f"list{k}") for k in range(4)]
+        planes = [sb.tile([P, POOL], U8, name=f"plane{k}", align_bytes=64) for k in range(3)]
+        keys_sb = sb.tile([P, 2 * POOL], U8, align_bytes=64)
+        notes_sb = sb.tile([P, POOL], U32, align_bytes=64)
+        users_sb = sb.tile([P, 2 * POOL], U8, align_bytes=64)
+        q_raw = sb.tile([P, PACK, Q], F32)
+        f1 = sb.tile([P, POOL], F32)
+
+        def load_scales(queue, plane, scales):
+            for quad in range(4):
+                queue.dma_start(out=plane[32 * quad:32 * quad + 4, :].bitcast(I32),
+                                in_=scales[0, 4 * quad:4 * quad + 4, :].bitcast(I32))
+
+        nc.vector.memset(f1[:], 0.0)
+
+        nc.sync.dma_start(out=q_raw[:], in_=query.rearrange("(p j) w -> p j w", j=PACK))
+        nc.sync.dma_start(out=keys_sb[:].bitcast(I32), in_=keys_words[0].bitcast(I32))
+        load_scales(nc.scalar, planes[0], keys_scales)
+        nc.sync.dma_start(out=notes_sb[:].bitcast(I32),
+                          in_=notes_words[0].rearrange("p n t -> p (n t)").bitcast(I32))
+        nc.sync.dma_start(out=users_sb[:].bitcast(I32), in_=users_words[0].bitcast(I32))
+        load_scales(nc.sync, planes[1], notes_scales)
+        load_scales(nc.gpsimd, planes[2], users_scales)
+        for tile_k, src_k in zip(lists, (offs, offs2, offs3, offs4)):
+            nc.sync.dma_start(tile_k[:], src_k)
+
+        q_bf = sb.tile([P, Q, PACK], BF16, align_bytes=64)
+        nc.vector.tensor_copy(out=q_bf[:].rearrange("p (c i) t -> p c t i", i=4),
+                              in_=q_raw[:].rearrange("p t (c i) -> p c t i", i=4))
+        q_codes = sb.tile([P, Q], U32, align_bytes=64)
+        q_scales = sb.tile([P, Q], U8, align_bytes=64)
+        nc.vector.quantize_mx(out=q_codes[:].bitcast(FP8X4), scales=q_scales[:],
+                              in_=q_bf[:].rearrange("p w j -> p (w j)"))
+
+        def words(k, h):
+            if k == 1:
+                return notes_sb[:, h * BANK:(h + 1) * BANK].bitcast(FP8X4)
+            packed = keys_sb if k == 0 else users_sb
+            return packed[:, 2 * h * BANK:2 * (h + 1) * BANK].bitcast(FP4X4)
+
+        banks = {}
+        for k in range(3):
+            for h in range(2):
+                bank = ps.tile([P, BANK], F32, name=f"bank{k}{h}")
+                nc.tensor.matmul_mx(out=bank[:], lhsT=q_codes[:].bitcast(FP8X4), lhsT_scale=q_scales[:],
+                                    rhs=words(k, h), rhs_scale=planes[k][:, h * BANK:(h + 1) * BANK],
+                                    start=True, stop=True)
+                banks[k, h] = bank
+
+        scores = [sb.tile([P, POOL], F32, name=f"scores{k}") for k in range(3)]
+        picked = {(k, h): sb.tile([P, HALF], F32, name=f"picked{k}{h}") for k in range(3) for h in range(2)}
+
+        def half_list(k, h):
+            return lists[k][:, h * LIST_COLS:(h + 1) * LIST_COLS]
+
+        def v_copy(k, h):
+            nc.vector.tensor_copy(out=scores[k][:, h * BANK:(h + 1) * BANK], in_=banks[k, h][:])
+
+        def s_copy(k, h):
+            nc.scalar.activation(scores[k][:, h * BANK:(h + 1) * BANK], banks[k, h][:], COPY)
+
+        def v_pick(k, h):
+            nc.vector.tensor_copy(picked[k, h][:], scores[k][:].indirect(half_list(k, h)))
+
+        def s_pick(k, h):
+            nc.scalar.activation(picked[k, h][:], scores[k][:].indirect(half_list(k, h)), COPY)
+
+        lo = [sb.tile([P, HALF], F32, name=f"lo{h}") for h in range(2)]
+        hi = [sb.tile([P, HALF], F32, name=f"hi{h}") for h in range(2)]
+        capped = [sb.tile([P, HALF], F32, name=f"capped{h}") for h in range(2)]
+        w_all = sb.tile([P, SLOTS], F32)
+        w = [w_all[:, h * HALF:(h + 1) * HALF] for h in range(2)]
+
+        def do_lo(h):
+            nc.vector.tensor_tensor(lo[h][:], picked[0, h][:], picked[1, h][:], ALU.min)
+
+        def do_hi(h):
+            nc.vector.tensor_tensor(hi[h][:], picked[0, h][:], picked[1, h][:], ALU.max)
+
+        def do_cap(h):
+            nc.vector.tensor_tensor(capped[h][:], hi[h][:], picked[2, h][:], ALU.min)
+
+        def do_w(h):
+            nc.vector.tensor_tensor(w[h], lo[h][:], capped[h][:], ALU.max)
+
+        v_copy(0, 0)
+        s_copy(0, 1)
+        v_pick(0, 0)
+        v_pick(0, 1)
+        s_copy(1, 0)
+        s_copy(1, 1)
+        s_copy(2, 0)
+        s_copy(2, 1)
+        v_pick(1, 0)
+        v_pick(1, 1)
+        s_pick(2, 0)
+        s_pick(2, 1)
+        do_hi(0)
+        do_lo(0)
+        do_hi(1)
+        do_lo(1)
+        do_cap(0)
+        do_cap(1)
+        do_w(0)
+        do_w(1)
+        nc.vector.tensor_copy(f1[:].indirect(lists[2][:]), w_all[:])
+
+        cc = sb.tile([P, POOL], F32)
+        nc.vector.tensor_tensor(cc[:], scores[2][:], f1[:], ALU.subtract)
+
+        res = [sb.tile([P, HALF], F32, name=f"res{h}") for h in range(2)]
+        left = sb.tile([P, HALF], F32)
+        nc.vector.tensor_tensor(res[0][:], cc[:].indirect(half_list(3, 0)), w[0], ALU.add)
+        nc.scalar.activation(left[:], cc[:].indirect(half_list(3, 1)), COPY)
+        nc.sync.dma_start(out=out[:, 0:HALF], in_=res[0][:])
+        nc.vector.tensor_tensor(res[1][:], left[:], w[1], ALU.add)
+        nc.sync.dma_start(out=out[:, HALF:SLOTS], in_=res[1][:])

@@ -38,99 +38,110 @@ def tile_attend_middleone_three_kernel(tc, query, keys_words, keys_scales, notes
         q_raw = sb.tile([P, PACK, Q], F32)
         f1 = sb.tile([P, POOL], F32)
 
-        def load_scales(queue, plane, scales):
-            for quad in range(4):
-                queue.dma_start(out=plane[32 * quad:32 * quad + 4, :].bitcast(I32),
+        def load_scales(queue, k, scales, quads):
+            for quad in quads:
+                queue.dma_start(out=planes[k][32 * quad:32 * quad + 4, :].bitcast(I32),
                                 in_=scales[0, 4 * quad:4 * quad + 4, :].bitcast(I32))
 
         nc.vector.memset(f1[:], 0.0)
 
         nc.sync.dma_start(out=q_raw[:], in_=query.rearrange("(p j) w -> p j w", j=PACK))
+        load_scales(nc.gpsimd, 2, users_scales, range(3, 4))
+        load_scales(nc.gpsimd, 1, notes_scales, range(3, 4))
+        load_scales(nc.sync, 0, keys_scales, range(2))
+        load_scales(nc.scalar, 0, keys_scales, range(2, 4))
+        load_scales(nc.scalar, 2, users_scales, range(1))
         nc.sync.dma_start(out=keys_sb[:].bitcast(I32), in_=keys_words[0].bitcast(I32))
-        load_scales(nc.scalar, planes[0], keys_scales)
+        nc.sync.dma_start(out=users_sb[:].bitcast(I32), in_=users_words[0].bitcast(I32))
+        load_scales(nc.sync, 2, users_scales, range(1, 3))
+        nc.sync.dma_start(lists[0][:], offs)
         nc.sync.dma_start(out=notes_sb[:].bitcast(I32),
                           in_=notes_words[0].rearrange("p n t -> p (n t)").bitcast(I32))
-        nc.sync.dma_start(out=users_sb[:].bitcast(I32), in_=users_words[0].bitcast(I32))
-        load_scales(nc.sync, planes[1], notes_scales)
-        load_scales(nc.gpsimd, planes[2], users_scales)
-        for tile_k, src_k in zip(lists, (offs, offs2, offs3, offs4)):
-            nc.sync.dma_start(tile_k[:], src_k)
+        load_scales(nc.sync, 1, notes_scales, range(3))
+        nc.sync.dma_start(lists[2][:], offs3)
+        nc.sync.dma_start(lists[1][:], offs2)
+        nc.sync.dma_start(lists[3][:], offs4)
 
-        q_bf = sb.tile([P, Q, PACK], BF16, align_bytes=64)
-        nc.vector.tensor_copy(out=q_bf[:].rearrange("p (c i) t -> p c t i", i=4),
-                              in_=q_raw[:].rearrange("p t (c i) -> p c t i", i=4))
         q_codes = sb.tile([P, Q], U32, align_bytes=64)
         q_scales = sb.tile([P, Q], U8, align_bytes=64)
-        nc.vector.quantize_mx(out=q_codes[:].bitcast(FP8X4), scales=q_scales[:],
-                              in_=q_bf[:].rearrange("p w j -> p (w j)"))
+        q_bf = [sb.tile([P, Q // 2, PACK], BF16, name=f"q_bf{h}", align_bytes=64) for h in range(2)]
 
-        def words(k, h):
+        def rows(h):
+            return q_raw[:, :, h * Q // 2:(h + 1) * Q // 2].rearrange("p t (c i) -> p c t i", i=4)
+
+        nc.vector.tensor_copy(out=q_bf[0][:].rearrange("p (c i) t -> p c t i", i=4), in_=rows(0))
+        nc.scalar.activation(q_bf[1][:].rearrange("p (c i) t -> p c t i", i=4), rows(1), COPY)
+        for h in range(2):
+            cols = slice(h * Q // 2, (h + 1) * Q // 2)
+            nc.vector.quantize_mx(out=q_codes[:, cols].bitcast(FP8X4), scales=q_scales[:, cols],
+                                  in_=q_bf[h][:].rearrange("p w j -> p (w j)"))
+
+        def words(k, c0, c1):
             if k == 1:
-                return notes_sb[:, h * BANK:(h + 1) * BANK].bitcast(FP8X4)
+                return notes_sb[:, c0:c1].bitcast(FP8X4)
             packed = keys_sb if k == 0 else users_sb
-            return packed[:, 2 * h * BANK:2 * (h + 1) * BANK].bitcast(FP4X4)
+            return packed[:, 2 * c0:2 * c1].bitcast(FP4X4)
 
+        cuts = {0: (0, 512, 768, 1024), 1: (0, 512, 1024), 2: (0, 512, 1024)}
         banks = {}
-        for k in range(3):
-            for h in range(2):
+        for k in (0, 2, 1):
+            for h, (c0, c1) in enumerate(zip(cuts[k], cuts[k][1:])):
                 bank = ps.tile([P, BANK], F32, name=f"bank{k}{h}")
-                nc.tensor.matmul_mx(out=bank[:], lhsT=q_codes[:].bitcast(FP8X4), lhsT_scale=q_scales[:],
-                                    rhs=words(k, h), rhs_scale=planes[k][:, h * BANK:(h + 1) * BANK],
+                nc.tensor.matmul_mx(out=bank[:, 0:c1 - c0], lhsT=q_codes[:].bitcast(FP8X4), lhsT_scale=q_scales[:],
+                                    rhs=words(k, c0, c1), rhs_scale=planes[k][:, c0:c1],
                                     start=True, stop=True)
-                banks[k, h] = bank
+                banks[k, h] = bank[:, 0:c1 - c0]
 
         scores = [sb.tile([P, POOL], F32, name=f"scores{k}") for k in range(3)]
-        picked = {(k, h): sb.tile([P, HALF], F32, name=f"picked{k}{h}") for k in range(3) for h in range(2)}
+        picked_all = [sb.tile([P, SLOTS], F32, name=f"picked{k}") for k in range(3)]
+        picked = {(k, h): picked_all[k][:, h * HALF:(h + 1) * HALF] for k in range(3) for h in range(2)}
 
         def half_list(k, h):
             return lists[k][:, h * LIST_COLS:(h + 1) * LIST_COLS]
 
         def v_copy(k, h):
-            nc.vector.tensor_copy(out=scores[k][:, h * BANK:(h + 1) * BANK], in_=banks[k, h][:])
+            nc.vector.tensor_copy(out=scores[k][:, cuts[k][h]:cuts[k][h + 1]], in_=banks[k, h])
 
         def s_copy(k, h):
-            nc.scalar.activation(scores[k][:, h * BANK:(h + 1) * BANK], banks[k, h][:], COPY)
+            nc.scalar.activation(scores[k][:, cuts[k][h]:cuts[k][h + 1]], banks[k, h], COPY)
 
         def v_pick(k, h):
-            nc.vector.tensor_copy(picked[k, h][:], scores[k][:].indirect(half_list(k, h)))
+            nc.vector.tensor_copy(picked[k, h], scores[k][:].indirect(half_list(k, h)))
 
         def s_pick(k, h):
-            nc.scalar.activation(picked[k, h][:], scores[k][:].indirect(half_list(k, h)), COPY)
+            nc.scalar.activation(picked[k, h], scores[k][:].indirect(half_list(k, h)), COPY)
 
-        lo = [sb.tile([P, HALF], F32, name=f"lo{h}") for h in range(2)]
+        lo_all = sb.tile([P, SLOTS], F32)
+        lo = [lo_all[:, h * HALF:(h + 1) * HALF] for h in range(2)]
         hi = [sb.tile([P, HALF], F32, name=f"hi{h}") for h in range(2)]
         capped = [sb.tile([P, HALF], F32, name=f"capped{h}") for h in range(2)]
         w_all = sb.tile([P, SLOTS], F32)
         w = [w_all[:, h * HALF:(h + 1) * HALF] for h in range(2)]
 
-        def do_lo(h):
-            nc.vector.tensor_tensor(lo[h][:], picked[0, h][:], picked[1, h][:], ALU.min)
-
         def do_hi(h):
-            nc.vector.tensor_tensor(hi[h][:], picked[0, h][:], picked[1, h][:], ALU.max)
+            nc.vector.tensor_tensor(hi[h][:], picked[0, h], picked[2, h], ALU.max)
 
         def do_cap(h):
-            nc.vector.tensor_tensor(capped[h][:], hi[h][:], picked[2, h][:], ALU.min)
+            nc.vector.tensor_tensor(capped[h][:], hi[h][:], picked[1, h], ALU.min)
 
         def do_w(h):
-            nc.vector.tensor_tensor(w[h], lo[h][:], capped[h][:], ALU.max)
+            nc.vector.tensor_tensor(w[h], lo[h], capped[h][:], ALU.max)
 
         v_copy(0, 0)
         s_copy(0, 1)
-        v_pick(0, 0)
-        v_pick(0, 1)
-        s_copy(1, 0)
-        s_copy(1, 1)
+        v_copy(0, 2)
         s_copy(2, 0)
         s_copy(2, 1)
-        v_pick(1, 0)
-        v_pick(1, 1)
-        s_pick(2, 0)
-        s_pick(2, 1)
+        nc.vector.tensor_copy(picked_all[0][:], scores[0][:].indirect(lists[0][:]))
+        s_copy(1, 0)
+        s_copy(1, 1)
+        v_pick(2, 0)
+        v_pick(2, 1)
+        s_pick(1, 0)
+        s_pick(1, 1)
         do_hi(0)
-        do_lo(0)
         do_hi(1)
-        do_lo(1)
+        nc.vector.tensor_tensor(lo_all[:], picked_all[0][:], picked_all[2][:], ALU.min)
         do_cap(0)
         do_cap(1)
         do_w(0)

@@ -149,7 +149,10 @@ def tile_attend_middleone_three_kernel(tc, query, keys_words, keys_scales, notes
         nc.vector.tensor_copy(f1[:].indirect(lists[2][:]), w_all[:])
 
         cc = sb.tile([P, POOL], F32)
-        nc.vector.tensor_tensor(cc[:], scores[2][:], f1[:], ALU.subtract)
+        split = 768
+        nc.gpsimd.tensor_tensor(cc[:, split:POOL], scores[2][:, split:POOL], f1[:, split:POOL], ALU.subtract)
+        nc.vector.tensor_tensor(cc[:, 0:BANK], banks[2, 0], f1[:, 0:BANK], ALU.subtract)
+        nc.vector.tensor_tensor(cc[:, BANK:split], banks[2, 1][:, 0:split - BANK], f1[:, BANK:split], ALU.subtract)
 
         res = [sb.tile([P, HALF], F32, name=f"res{h}") for h in range(2)]
         left = sb.tile([P, HALF], F32)

from contextlib import ExitStack

import concourse.mybir as mybir

D, POOL, SLOTS, Q = 512, 1024, 512, 128
FLOPS = 3 * 2 * D * Q * POOL

F32 = mybir.dt.float32
BF16 = mybir.dt.bfloat16
I32 = mybir.dt.int32
U32 = mybir.dt.uint32
U16 = mybir.dt.uint16
U8 = mybir.dt.uint8
FP8X4 = mybir.dt.float8_e4m3fn_x4
FP4X4 = mybir.dt.float4_e2m1fn_x4
COPY = mybir.ActivationFunctionType.Copy
ALU = mybir.AluOpType

P = 128
PACK = 4
BANK = 512
HALF = SLOTS // 2
LIST_COLS = HALF // 16


def tile_attend_middleone_three_kernel(tc, query, keys_words, keys_scales, notes_words, notes_scales,
                                        users_words, users_scales, offs, offs2, offs3, offs4, out):
    nc = tc.nc
    with ExitStack() as ctx:
        sb = ctx.enter_context(tc.tile_pool(name="sb", bufs=1))
        ps = ctx.enter_context(tc.psum_pool(name="ps", bufs=1))

        lists = [sb.tile([P, SLOTS // 16], U16, name=f"list{k}") for k in range(4)]
        planes = [sb.tile([P, POOL], U8, name=f"plane{k}", align_bytes=64) for k in range(3)]
        keys_sb = sb.tile([P, 2 * POOL], U8, align_bytes=64)
        notes_sb = sb.tile([P, POOL], U32, align_bytes=64)
        users_sb = sb.tile([P, 2 * POOL], U8, align_bytes=64)
        q_raw = sb.tile([P, PACK, Q], F32)
        f1 = sb.tile([P, POOL], F32)

        def load_scales(queue, k, scales, quads):
            for quad in quads:
                queue.dma_start(out=planes[k][32 * quad:32 * quad + 4, :].bitcast(I32),
                                in_=scales[0, 4 * quad:4 * quad + 4, :].bitcast(I32))

        nc.vector.memset(f1[:], 0.0)

        nc.sync.dma_start(out=q_raw[:], in_=query.rearrange("(p j) w -> p j w", j=PACK))
        load_scales(nc.gpsimd, 2, users_scales, range(3, 4))
        load_scales(nc.gpsimd, 1, notes_scales, range(3, 4))
        load_scales(nc.sync, 0, keys_scales, range(2))
        load_scales(nc.scalar, 0, keys_scales, range(2, 4))
        load_scales(nc.scalar, 2, users_scales, range(1))
        nc.sync.dma_start(out=keys_sb[:].bitcast(I32), in_=keys_words[0].bitcast(I32))
        nc.sync.dma_start(out=users_sb[:].bitcast(I32), in_=users_words[0].bitcast(I32))
        load_scales(nc.sync, 2, users_scales, range(1, 3))
        nc.sync.dma_start(lists[0][:], offs)
        nc.sync.dma_start(out=notes_sb[:].bitcast(I32),
                          in_=notes_words[0].rearrange("p n t -> p (n t)").bitcast(I32))
        load_scales(nc.sync, 1, notes_scales, range(3))
        nc.sync.dma_start(lists[2][:], offs3)
        nc.sync.dma_start(lists[1][:], offs2)
        nc.sync.dma_start(lists[3][:], offs4)

        q_codes = sb.tile([P, Q], U32, align_bytes=64)
        q_scales = sb.tile([P, Q], U8, align_bytes=64)
        q_bf = [sb.tile([P, Q // 2, PACK], BF16, name=f"q_bf{h}", align_bytes=64) for h in range(2)]

        def rows(h):
            return q_raw[:, :, h * Q // 2:(h + 1) * Q // 2].rearrange("p t (c i) -> p c t i", i=4)

        nc.vector.tensor_copy(out=q_bf[0][:].rearrange("p (c i) t -> p c t i", i=4), in_=rows(0))
        nc.scalar.activation(q_bf[1][:].rearrange("p (c i) t -> p c t i", i=4), rows(1), COPY)
        for h in range(2):
            cols = slice(h * Q // 2, (h + 1) * Q // 2)
            nc.vector.quantize_mx(out=q_codes[:, cols].bitcast(FP8X4), scales=q_scales[:, cols],
                                  in_=q_bf[h][:].rearrange("p w j -> p (w j)"))

        def words(k, c0, c1):
            if k == 1:
                return notes_sb[:, c0:c1].bitcast(FP8X4)
            packed = keys_sb if k == 0 else users_sb
            return packed[:, 2 * c0:2 * c1].bitcast(FP4X4)

        cuts = {0: (0, 512, 768, 1024), 1: (0, 512, 1024), 2: (0, 512, 1024)}
        banks = {}
        for k in (0, 2, 1):
            for h, (c0, c1) in enumerate(zip(cuts[k], cuts[k][1:])):
                bank = ps.tile([P, BANK], F32, name=f"bank{k}{h}")
                nc.tensor.matmul_mx(out=bank[:, 0:c1 - c0], lhsT=q_codes[:].bitcast(FP8X4), lhsT_scale=q_scales[:],
                                    rhs=words(k, c0, c1), rhs_scale=planes[k][:, c0:c1],
                                    start=True, stop=True)
                banks[k, h] = bank[:, 0:c1 - c0]

        scores = [sb.tile([P, POOL], F32, name=f"scores{k}") for k in range(3)]
        picked_all = [sb.tile([P, SLOTS], F32, name=f"picked{k}") for k in range(3)]
        picked = {(k, h): picked_all[k][:, h * HALF:(h + 1) * HALF] for k in range(3) for h in range(2)}

        def half_list(k, h):
            return lists[k][:, h * LIST_COLS:(h + 1) * LIST_COLS]

        def v_copy(k, h):
            nc.vector.tensor_copy(out=scores[k][:, cuts[k][h]:cuts[k][h + 1]], in_=banks[k, h])

        def s_copy(k, h):
            nc.scalar.activation(scores[k][:, cuts[k][h]:cuts[k][h + 1]], banks[k, h], COPY)

        def v_pick(k, h):
            nc.vector.tensor_copy(picked[k, h], scores[k][:].indirect(half_list(k, h)))

        def s_pick(k, h):
            nc.scalar.activation(picked[k, h], scores[k][:].indirect(half_list(k, h)), COPY)

        lo_all = sb.tile([P, SLOTS], F32)
        lo = [lo_all[:, h * HALF:(h + 1) * HALF] for h in range(2)]
        hi = [sb.tile([P, HALF], F32, name=f"hi{h}") for h in range(2)]
        capped = [sb.tile([P, HALF], F32, name=f"capped{h}") for h in range(2)]
        w_all = sb.tile([P, SLOTS], F32)
        w = [w_all[:, h * HALF:(h + 1) * HALF] for h in range(2)]

        def do_hi(h):
            nc.vector.tensor_tensor(hi[h][:], picked[0, h], picked[2, h], ALU.max)

        def do_cap(h):
            nc.vector.tensor_tensor(capped[h][:], hi[h][:], picked[1, h], ALU.min)

        def do_w(h):
            nc.vector.tensor_tensor(w[h], lo[h], capped[h][:], ALU.max)

        v_copy(0, 0)
        s_copy(0, 1)
        v_copy(0, 2)
        s_copy(2, 0)
        s_copy(2, 1)
        nc.vector.tensor_copy(picked_all[0][:], scores[0][:].indirect(lists[0][:]))
        s_copy(1, 0)
        s_copy(1, 1)
        v_pick(2, 0)
        v_pick(2, 1)
        s_pick(1, 0)
        s_pick(1, 1)
        do_hi(0)
        do_hi(1)
        nc.vector.tensor_tensor(lo_all[:], picked_all[0][:], picked_all[2][:], ALU.min)
        do_cap(0)
        do_cap(1)
        do_w(0)
        do_w(1)
        nc.vector.tensor_copy(f1[:].indirect(lists[2][:]), w_all[:])

        cc = sb.tile([P, POOL], F32)
        split = 768
        nc.gpsimd.tensor_tensor(cc[:, split:POOL], scores[2][:, split:POOL], f1[:, split:POOL], ALU.subtract)
        nc.vector.tensor_tensor(cc[:, 0:BANK], banks[2, 0], f1[:, 0:BANK], ALU.subtract)
        nc.vector.tensor_tensor(cc[:, BANK:split], banks[2, 1][:, 0:split - BANK], f1[:, BANK:split], ALU.subtract)

        res = [sb.tile([P, HALF], F32, name=f"res{h}") for h in range(2)]
        left = sb.tile([P, HALF], F32)
        nc.vector.tensor_tensor(res[0][:], cc[:].indirect(half_list(3, 0)), w[0], ALU.add)
        nc.scalar.activation(left[:], cc[:].indirect(half_list(3, 1)), COPY)
        nc.sync.dma_start(out=out[:, 0:HALF], in_=res[0][:])
        nc.vector.tensor_tensor(res[1][:], left[:], w[1], ALU.add)
        nc.sync.dma_start(out=out[:, HALF:SLOTS], in_=res[1][:])
